import numpy as np
import ml_dtypes


def mxq(x, axis, fmt="e4m3"):
    dtype, down = {"e4m3": (ml_dtypes.float8_e4m3fn, 7), "e5m2": (ml_dtypes.float8_e5m2, 14)}[fmt]
    v = np.moveaxis(np.asarray(x, np.float32).astype(ml_dtypes.bfloat16).astype(np.float64), axis, -1)
    blocks = v.reshape(v.shape[:-1] + (-1, 32))
    amax = np.abs(blocks).max(-1, keepdims=True)
    byte = np.maximum(np.where(amax > 0, np.frexp(amax)[1] - 1 + 127, 0) - down, 1)
    scale = np.exp2(byte - 127.0)
    codes = (blocks / scale).astype(np.float32).astype(dtype).astype(np.float64)
    return np.moveaxis((codes * scale).reshape(v.shape), -1, axis)


WIDE = False


def mx_kscale(k):
    if not WIDE:
        return np.ones(k)
    levels = np.array([10, -10, 5, -5, 0])
    if k % 512:
        return np.exp2(np.random.permutation(np.resize(levels, k // 32))).repeat(32)
    a = np.empty((k // 512, 16))
    for p in range(k // 512):
        a[p, :8] = np.random.permutation(np.resize(levels, 8))
        for g in range(8):
            far = levels[np.abs(levels - a[p, g]) >= 10]
            a[p, g + 8] = far[np.random.randint(len(far))]
    return np.exp2(a.ravel()).repeat(32)


BF16 = ml_dtypes.bfloat16


def bf(x):
    return np.asarray(x, np.float32).astype(BF16)


def f64(x):
    return np.asarray(x).astype(np.float64)

E4M3FN = np.array([(-1.0 if i & 128 else 1.0) * ((1.0 + (i & 7) / 8.0) * 2.0 ** (((i >> 3) & 15) - 7) if i & 120 else (i & 7) * 2.0 ** -9) for i in range(256)])


def e4m3fn_bytes(y):
    return np.clip(np.asarray(y, np.float64), -448.0, 448.0).astype(np.float32).astype(ml_dtypes.float8_e4m3fn).view(np.uint8)


def e4m3fn_values(b):
    return E4M3FN[b]


N, K, J = 1536, 512, 1024


def setup_inputs():
    s, t = mx_kscale(K), mx_kscale(J)
    a = np.random.standard_normal((K, N)) * np.exp(0.3 * np.random.standard_normal((K, 1))) * s[:, None]
    b = np.random.standard_normal((J, N)) * np.exp(0.3 * np.random.standard_normal((J, 1))) / np.sqrt(J) * t[:, None]
    a_scale = (np.abs(a).max(axis=1, keepdims=True) / 448).astype(np.float32)
    b_scale = (np.abs(b).max(axis=1, keepdims=True) / 448).astype(np.float32)
    return {"A_bytes": e4m3fn_bytes(a / f64(a_scale)),
            "A_scale": a_scale,
            "B_bytes": e4m3fn_bytes(b / f64(b_scale)),
            "B_scale": b_scale,
            "F": bf(np.random.standard_normal((K, J)) / np.sqrt(K) / s[:, None] / t),
            "v": bf(1 + 0.1 * np.random.standard_normal(J)),
            "d": bf(2 + np.abs(np.random.standard_normal(N)))}


def reference(A_bytes, A_scale, B_bytes, B_scale, F, v, d):
    a = mxq(e4m3fn_values(A_bytes) * np.repeat(f64(A_scale), N, axis=1), 0, "e4m3")
    b = mxq(e4m3fn_values(B_bytes) * np.repeat(f64(B_scale), N, axis=1), 0, "e4m3")
    g = (a.T @ mxq(f64(F), 0, "e4m3")) * f64(v)
    c = mxq(g, 1, "e4m3") @ b
    return c + np.eye(N) * f64(d)

@@ -1,0 +1,355 @@
+from contextlib import ExitStack
+
+import concourse.mybir as mybir
+from concourse.masks import make_identity
+
+N, K, J = 1536, 512, 1024
+FLOPS = 2 * (N * K * J + N * J * N)
+
+F32 = mybir.dt.float32
+BF16 = mybir.dt.bfloat16
+U32 = mybir.dt.uint32
+U8 = mybir.dt.uint8
+E4M3 = mybir.dt.float8_e4m3fn
+FP8X4 = mybir.dt.float8_e4m3fn_x4
+MULT = mybir.AluOpType.mult
+ADD = mybir.AluOpType.add
+COPY = mybir.ActivationFunctionType.Copy
+
+P = 128
+T = 4
+CH = 512
+NCH = N // CH
+PASSES = J // (P * T)
+SUB = CH // P
+MT = N // P
+
+MANUAL = False
+NPL = 8
+SEQ = [
+    ('WA', 0, 256, 'M'),
+    ('IA', 0, 256, 'V'),
+    ('IF', 0, 'V'),
+    ('QA', 0, 256),
+    ('QF', 0),
+    ('IF', 1, 'V'),
+    ('QF', 1),
+    ('G', 0),
+    ('G', 1),
+    ('QG', 0),
+    ('QG', 1),
+    ('D',),
+    ('WB', 0, 0, 512, 'S'),
+    ('WB', 1, 0, 512, 'V'),
+    ('WB', 0, 512, 512, 'S'),
+    ('WB', 1, 512, 512, 'V'),
+    ('WA', 256, 256, 'S'),
+    ('PB', 0, 0, 512, 'S'),
+    ('PB', 1, 0, 512, 'S'),
+    ('QB', 0, 0, 512),
+    ('QB', 1, 0, 512),
+    ('WB', 0, 1024, 512, 'S'),
+    ('WB', 1, 1024, 512, 'V'),
+    ('PB', 0, 512, 512, 'S'),
+    ('PB', 1, 512, 512, 'S'),
+    ('QB', 0, 512, 512),
+    ('QB', 1, 512, 512),
+    ('O', 0, 0, 512, 'S'),
+    ('O', 1, 0, 512, 'S'),
+    ('WA', 512, 128, 'S'),
+    ('IA', 256, 256, 'V'),
+    ('QA', 256, 256),
+    ('G', 2),
+    ('G', 3),
+    ('QG', 2),
+    ('QG', 3),
+    ('O', 0, 512, 512, 'S'),
+    ('O', 1, 512, 512, 'S'),
+    ('WA', 640, 128, 'S'),
+    ('PB', 0, 1024, 512, 'S'),
+    ('PB', 1, 1024, 512, 'S'),
+    ('QB', 0, 1024, 512),
+    ('QB', 1, 1024, 512),
+    ('O', 2, 0, 512, 'S'),
+    ('O', 2, 512, 512, 'S'),
+    ('O', 3, 0, 512, 'S'),
+    ('O', 3, 512, 512, 'S'),
+    ('WA', 768, 128, 'S'),
+    ('IA', 512, 128, 'V'),
+    ('QA', 512, 128),
+    ('G', 4),
+    ('QG', 4),
+    ('O', 0, 1024, 512, 'S'),
+    ('O', 1, 1024, 512, 'S'),
+    ('O', 2, 1024, 512, 'S'),
+    ('O', 3, 1024, 512, 'S'),
+    ('WA', 896, 128, 'S'),
+    ('IA', 640, 128, 'V'),
+    ('QA', 640, 128),
+    ('G', 5),
+    ('QG', 5),
+    ('O', 4, 0, 512, 'S'),
+    ('O', 4, 512, 512, 'S'),
+    ('O', 4, 1024, 512, 'S'),
+    ('WA', 1024, 128, 'S'),
+    ('IA', 768, 128, 'V'),
+    ('QA', 768, 128),
+    ('G', 6),
+    ('QG', 6),
+    ('O', 5, 0, 512, 'S'),
+    ('O', 5, 512, 512, 'S'),
+    ('O', 5, 1024, 512, 'S'),
+    ('WA', 1152, 128, 'S'),
+    ('IA', 896, 128, 'V'),
+    ('QA', 896, 128),
+    ('G', 7),
+    ('QG', 7),
+    ('O', 6, 0, 512, 'S'),
+    ('O', 6, 512, 512, 'S'),
+    ('O', 6, 1024, 512, 'S'),
+    ('WA', 1280, 128, 'S'),
+    ('IA', 1024, 128, 'V'),
+    ('QA', 1024, 128),
+    ('G', 8),
+    ('QG', 8),
+    ('O', 7, 512, 512, 'S'),
+    ('O', 7, 0, 512, 'S'),
+    ('O', 7, 1024, 512, 'S'),
+    ('WA', 1408, 128, 'S'),
+    ('IA', 1152, 128, 'V'),
+    ('QA', 1152, 128),
+    ('G', 9),
+    ('QG', 9),
+    ('O', 8, 1024, 512, 'S'),
+    ('O', 8, 0, 512, 'S'),
+    ('O', 8, 512, 512, 'S'),
+    ('IA', 1280, 128, 'V'),
+    ('QA', 1280, 128),
+    ('G', 10),
+    ('QG', 10),
+    ('O', 9, 1024, 512, 'S'),
+    ('O', 9, 0, 512, 'S'),
+    ('O', 9, 512, 512, 'S'),
+    ('IA', 1408, 128, 'V'),
+    ('QA', 1408, 128),
+    ('G', 11),
+    ('QG', 11),
+    ('O', 10, 1024, 512, 'S'),
+    ('O', 10, 0, 512, 'S'),
+    ('O', 10, 512, 512, 'S'),
+    ('O', 11, 1024, 512, 'S'),
+    ('O', 11, 0, 512, 'S'),
+    ('O', 11, 512, 256, 'V'),
+    ('O', 11, 768, 256, 'S'),
+]
+
+
+def tile_listing_cross_covariance_d5_kernel(
+    tc, A_bytes, A_scale, B_bytes, B_scale, F, v, d, out
+):
+    nc = tc.nc
+    with ExitStack() as ctx:
+        keep = ctx.enter_context(tc.tile_pool(name="keep", bufs=1))
+        work = ctx.enter_context(tc.tile_pool(name="work", bufs=4))
+        outs = ctx.enter_context(tc.tile_pool(name="outs", bufs=12))
+        ps = ctx.enter_context(tc.psum_pool(name="ps", bufs=4))
+
+        a_by = keep.tile([P, T, N], U8, name="a_by", align_bytes=64)
+        b_by = keep.tile([P, PASSES, T, N], U8, name="b_by", align_bytes=64)
+        f_raw = keep.tile([P, T, J], BF16, name="f_raw", align_bytes=64)
+        a_sc = keep.tile([P, T], F32, name="a_sc")
+        b_sc = keep.tile([P, PASSES, T], F32, name="b_sc")
+        v_sb = keep.tile([P, PASSES, T], BF16, name="v_sb")
+        d_rows = keep.tile([P, P], BF16, name="d_rows")
+        d_col = keep.tile([P, MT], F32, name="d_col")
+        ident = keep.tile([P, P], BF16, name="ident")
+
+        a_cod = keep.tile([P, N], U32, name="a_cod", align_bytes=64)
+        a_qs = keep.tile([P, N], U8, name="a_qs", align_bytes=64)
+        f_cod = keep.tile([P, J], U32, name="f_cod", align_bytes=64)
+        f_qs = keep.tile([P, J], U8, name="f_qs", align_bytes=64)
+        b_cod = keep.tile([P, PASSES, N], U32, name="b_cod", align_bytes=64)
+        b_qs = keep.tile([P, PASSES, N], U8, name="b_qs", align_bytes=64)
+        g_cod = keep.tile([P, MT, PASSES * P], U32, name="g_cod", align_bytes=64)
+        g_qs = keep.tile([P, MT, PASSES * P], U8, name="g_qs", align_bytes=64)
+
+        a_hbm = A_bytes.rearrange("(p t) n -> p t n", t=T)
+        b_hbm = B_bytes.rearrange("(g p t) n -> g p t n", p=P, t=T)
+        f_hbm = F.rearrange("(p t) j -> p t j", t=T)
+        nc.sync.dma_start(out=a_sc[:], in_=A_scale.rearrange("(p t) o -> p (t o)", t=T))
+        nc.sync.dma_start(out=a_by[:, :, 0:CH], in_=a_hbm[:, :, 0:CH])
+        nc.sync.dma_start(out=f_raw[:, :, 0:CH], in_=f_hbm[:, :, 0:CH])
+        nc.sync.dma_start(out=f_raw[:, :, CH:J], in_=f_hbm[:, :, CH:J])
+        nc.sync.dma_start(out=b_sc[:], in_=B_scale.rearrange("(g p t) o -> p g (t o)", p=P, t=T))
+        nc.sync.dma_start(out=v_sb[:], in_=v.rearrange("(g p t) -> p g t", p=P, t=T))
+        for g in range(PASSES):
+            for h in range(2):
+                nc.sync.dma_start(
+                    out=b_by[:, g, 2 * h : 2 * h + 2, :], in_=b_hbm[g, :, 2 * h : 2 * h + 2, :]
+                )
+        nc.sync.dma_start(out=a_by[:, :, CH:N], in_=a_hbm[:, :, CH:N])
+        nc.vector.memset(d_rows[:], 0.0)
+        make_identity(nc, ident[:])
+        nc.gpsimd.dma_start(out=d_rows[0:MT, :], in_=d.rearrange("(c p) -> c p", p=P))
+
+        planes = {}
+        mixed = {}
+
+        def widen(key, src, scale, w, eng):
+            pl = work.tile([P, T, w], BF16, name="pl" + str(w), bufs=NPL, align_bytes=64)
+            planes[key] = pl
+            for t in range(T):
+                if eng == "S" or (eng == "M" and t % 2):
+                    nc.scalar.activation(
+                        out=pl[:, t, :], in_=src[:, t, :].bitcast(E4M3), func=COPY, scale=scale[:, t : t + 1]
+                    )
+                else:
+                    nc.vector.tensor_scalar(
+                        out=pl[:, t, :], in0=src[:, t, :].bitcast(E4M3), scalar1=scale[:, t : t + 1], scalar2=None, op0=MULT
+                    )
+
+        def inter(key, w, eng):
+            x = work.tile([P, T * w], BF16, name="ix" + str(w), align_bytes=64)
+            mixed[key] = x
+            o = x[:].rearrange("p (n t) -> p n t", t=T)
+            i = planes[key][:].rearrange("p t n -> p n t")
+            if eng == "S":
+                nc.scalar.copy(out=o, in_=i)
+            else:
+                nc.vector.tensor_copy(out=o, in_=i)
+
+        def pe_inter(key, w, eng):
+            x = work.tile([P, T * w], BF16, name="ix" + str(w), align_bytes=64)
+            mixed[key] = x
+            pl = planes[key]
+            for h in range(w // 256):
+                bank = ps.tile([P, 2 * CH], BF16, name="gb")
+                for q in range(2):
+                    n0 = h * 256 + q * P
+                    nc.tensor.matmul(
+                        out=bank[:, q * CH : (q + 1) * CH],
+                        lhsT=ident[:],
+                        rhs=pl[:, :, n0 : n0 + P].rearrange("p t n -> p n t"),
+                        start=True,
+                        stop=True,
+                    )
+                o = x[:, h * 2 * CH : (h + 1) * 2 * CH]
+                e = eng[h % len(eng)]
+                if e == "S":
+                    nc.scalar.copy(out=o, in_=bank[:])
+                else:
+                    nc.vector.tensor_copy(out=o, in_=bank[:])
+
+        def quant(cod, qs, src):
+            nc.vector.quantize_mx(out=cod.bitcast(FP8X4), scales=qs, in_=src[:])
+
+        def f_inter(g, eng):
+            x = work.tile([P, T * CH], BF16, name="fx", bufs=2, align_bytes=64)
+            mixed["F", g] = x
+            o = x[:].rearrange("p (t m j) -> p t m j", t=T, j=T)
+            i = f_raw[:, :, g * CH : (g + 1) * CH].rearrange("p j (m t) -> p t m j", t=T)
+            if eng == "S":
+                nc.scalar.copy(out=o, in_=i)
+            else:
+                nc.vector.tensor_copy(out=o, in_=i)
+
+        gx = {}
+
+        def g_mm(mt):
+            x = work.tile([P, PASSES * T * P], BF16, name="gx", align_bytes=64)
+            gx[mt] = x
+            i0 = mt * P
+            for g in range(PASSES):
+                bank = ps.tile([P, T, P], F32, name="gb")
+                for t in range(T):
+                    j0 = (g * T + t) * P
+                    nc.tensor.matmul_mx(
+                        out=bank[:, t, :],
+                        lhsT=f_cod[:, j0 : j0 + P].bitcast(FP8X4),
+                        lhsT_scale=f_qs[:, j0 : j0 + P],
+                        rhs=a_cod[:, i0 : i0 + P].bitcast(FP8X4),
+                        rhs_scale=a_qs[:, i0 : i0 + P],
+                        start=True,
+                        stop=True,
+                    )
+                nc.vector.tensor_tensor(
+                    out=x[:, g * CH : (g + 1) * CH].rearrange("p (n t) -> p n t", t=T),
+                    in0=bank[:].rearrange("p t n -> p n t"),
+                    in1=v_sb[:, g : g + 1, :].to_broadcast([P, P, T]),
+                    op=MULT,
+                )
+
+        def g_q(mt):
+            quant(g_cod[:, mt, :], g_qs[:, mt, :], gx[mt])
+
+        def out_mm(mt, c0, w, eng):
+            bank = ps.tile([P, CH], F32, name="ob")
+            for g in range(PASSES):
+                nc.tensor.matmul_mx(
+                    out=bank[:, 0:w],
+                    lhsT=g_cod[:, mt, g * P : (g + 1) * P].bitcast(FP8X4),
+                    lhsT_scale=g_qs[:, mt, g * P : (g + 1) * P],
+                    rhs=b_cod[:, g, c0 : c0 + w].bitcast(FP8X4),
+                    rhs_scale=b_qs[:, g, c0 : c0 + w],
+                    start=(g == 0),
+                    stop=(g == PASSES - 1),
+                )
+            o = outs.tile([P, w], F32, name="o" + str(w))
+            if eng == "S":
+                nc.scalar.copy(out=o[:], in_=bank[:, 0:w])
+            else:
+                nc.vector.tensor_copy(out=o[:], in_=bank[:, 0:w])
+            x0 = mt * P - c0
+            if 0 <= x0 < w:
+                nc.vector.scalar_tensor_tensor(
+                    out=o[:, x0 : x0 + P],
+                    in0=ident[:],
+                    scalar=d_col[:, mt : mt + 1],
+                    in1=o[:, x0 : x0 + P],
+                    op0=MULT,
+                    op1=ADD,
+                )
+            nc.sync.dma_start(out=out[mt * P : (mt + 1) * P, c0 : c0 + w], in_=o[:])
+
+        def d_setup():
+            dp = ps.tile([P, P], BF16, name="gb")
+            nc.tensor.transpose(dp[:], d_rows[:], ident[:])
+            nc.vector.tensor_copy(out=d_col[:], in_=dp[:, 0:MT])
+
+        def run():
+            for s in SEQ:
+                k = s[0]
+                if k == "WA":
+                    widen(("A", s[1]), a_by[:, :, s[1] : s[1] + s[2]], a_sc, s[2], s[3])
+                elif k == "WB":
+                    widen(("B", s[1], s[2]), b_by[:, s[1], :, s[2] : s[2] + s[3]], b_sc[:, s[1], :], s[3], s[4])
+                elif k == "IA":
+                    inter(("A", s[1]), s[2], s[3])
+                elif k == "IB":
+                    inter(("B", s[1], s[2]), s[3], s[4])
+                elif k == "PB":
+                    pe_inter(("B", s[1], s[2]), s[3], s[4])
+                elif k == "PA":
+                    pe_inter(("A", s[1]), s[2], s[3])
+                elif k == "QA":
+                    quant(a_cod[:, s[1] : s[1] + s[2]], a_qs[:, s[1] : s[1] + s[2]], mixed["A", s[1]])
+                elif k == "QB":
+                    quant(b_cod[:, s[1], s[2] : s[2] + s[3]], b_qs[:, s[1], s[2] : s[2] + s[3]], mixed["B", s[1], s[2]])
+                elif k == "IF":
+                    f_inter(s[1], s[2])
+                elif k == "QF":
+                    quant(f_cod[:, s[1] * CH : (s[1] + 1) * CH], f_qs[:, s[1] * CH : (s[1] + 1) * CH], mixed["F", s[1]])
+                elif k == "G":
+                    g_mm(s[1])
+                elif k == "QG":
+                    g_q(s[1])
+                elif k == "D":
+                    d_setup()
+                elif k == "O":
+                    out_mm(s[1], s[2], s[3], s[4])
+
+        if MANUAL:
+            with tc.manual_schedule():
+                run()
+        else:
+            run()

@@ -40,18 +40,18 @@ SEQ = [
     ('QG', 1),
     ('D',),
     ('WB', 0, 0, 512, 'S'),
-    ('WB', 1, 0, 512, 'V'),
+    ('WB', 1, 0, 512, 'S'),
     ('WB', 0, 512, 512, 'S'),
-    ('WB', 1, 512, 512, 'V'),
+    ('WB', 1, 512, 512, 'S'),
     ('WA', 256, 256, 'S'),
-    ('PB', 0, 0, 512, 'S'),
-    ('PB', 1, 0, 512, 'S'),
+    ('IB', 0, 0, 512, 'V'),
+    ('IB', 1, 0, 512, 'V'),
     ('QB', 0, 0, 512),
     ('QB', 1, 0, 512),
     ('WB', 0, 1024, 512, 'S'),
-    ('WB', 1, 1024, 512, 'V'),
-    ('PB', 0, 512, 512, 'S'),
-    ('PB', 1, 512, 512, 'S'),
+    ('WB', 1, 1024, 512, 'S'),
+    ('IB', 0, 512, 512, 'V'),
+    ('IB', 1, 512, 512, 'V'),
     ('QB', 0, 512, 512),
     ('QB', 1, 512, 512),
     ('O', 0, 0, 512, 'S'),
@@ -66,8 +66,8 @@ SEQ = [
     ('O', 0, 512, 512, 'S'),
     ('O', 1, 512, 512, 'S'),
     ('WA', 640, 128, 'S'),
-    ('PB', 0, 1024, 512, 'S'),
-    ('PB', 1, 1024, 512, 'S'),
+    ('IB', 0, 1024, 512, 'V'),
+    ('IB', 1, 1024, 512, 'V'),
     ('QB', 0, 1024, 512),
     ('QB', 1, 1024, 512),
     ('O', 2, 0, 512, 'S'),

@@ -211,8 +211,8 @@ def tile_listing_cross_covariance_d5_kernel(
         def inter(key, w, eng):
             x = work.tile([P, T * w], BF16, name="ix" + str(w), align_bytes=64)
             mixed[key] = x
-            o = x[:].rearrange("p (n t) -> p n t", t=T)
-            i = planes[key][:].rearrange("p t n -> p n t")
+            o = x[:].rearrange("p (c i t) -> p c t i", i=4, t=T)
+            i = planes[key][:].rearrange("p t (c i) -> p c t i", i=4)
             if eng == "S":
                 nc.scalar.copy(out=o, in_=i)
             else:
@@ -273,9 +273,9 @@ def tile_listing_cross_covariance_d5_kernel(
                         stop=True,
                     )
                 nc.vector.tensor_tensor(
-                    out=x[:, g * CH : (g + 1) * CH].rearrange("p (n t) -> p n t", t=T),
-                    in0=bank[:].rearrange("p t n -> p n t"),
-                    in1=v_sb[:, g : g + 1, :].to_broadcast([P, P, T]),
+                    out=x[:, g * CH : (g + 1) * CH].rearrange("p (c i t) -> p c t i", i=4, t=T),
+                    in0=bank[:].rearrange("p t (c i) -> p c t i", i=4),
+                    in1=v_sb[:, g : g + 1, :].unsqueeze(3).to_broadcast([P, P // 4, T, 4]),
                     op=MULT,
                 )
 

@@ -18,129 +18,282 @@ COPY = mybir.ActivationFunctionType.Copy
 
 P = 128
 T = 4
-CH = 512
-NCH = N // CH
-PASSES = J // (P * T)
-SUB = CH // P
+G = J // (P * T)
 MT = N // P
+BANK = 512
+HALF = N // 2
+WHOLE_ROWS_FROM = 6
 
 MANUAL = False
-NPL = 8
+A_CHUNKS = [(0, 256), (256, 256), (512, 128), (640, 128), (768, 128), (896, 128), (1024, 128), (1152, 128), (1280, 128), (1408, 128)]
+B_CHUNKS = [(0, 512), (512, 512), (1024, 512)]
+TWO_INPUT = [256, 512, 640, 768, 896, 1024, 1152, 1280, 1408]
 SEQ = [
-    ('WA', 0, 256, 'M'),
-    ('IA', 0, 256, 'V'),
-    ('IF', 0, 'V'),
-    ('QA', 0, 256),
-    ('QF', 0),
-    ('IF', 1, 'V'),
-    ('QF', 1),
-    ('G', 0),
-    ('G', 1),
-    ('QG', 0),
-    ('QG', 1),
-    ('D',),
-    ('WB', 0, 0, 512, 'S'),
-    ('WB', 1, 0, 512, 'S'),
-    ('WB', 0, 512, 512, 'S'),
-    ('WB', 1, 512, 512, 'S'),
-    ('WA', 256, 256, 'S'),
-    ('IB', 0, 0, 512, 'V'),
-    ('IB', 1, 0, 512, 'V'),
-    ('QB', 0, 0, 512),
-    ('QB', 1, 0, 512),
-    ('WB', 0, 1024, 512, 'S'),
-    ('WB', 1, 1024, 512, 'S'),
-    ('IB', 0, 512, 512, 'V'),
-    ('IB', 1, 512, 512, 'V'),
-    ('QB', 0, 512, 512),
-    ('QB', 1, 512, 512),
-    ('O', 0, 0, 512, 'S'),
-    ('O', 1, 0, 512, 'S'),
-    ('WA', 512, 128, 'S'),
-    ('IA', 256, 256, 'V'),
-    ('QA', 256, 256),
-    ('G', 2),
-    ('G', 3),
-    ('QG', 2),
-    ('QG', 3),
-    ('O', 0, 512, 512, 'S'),
-    ('O', 1, 512, 512, 'S'),
-    ('WA', 640, 128, 'S'),
-    ('IB', 0, 1024, 512, 'V'),
-    ('IB', 1, 1024, 512, 'V'),
-    ('QB', 0, 1024, 512),
-    ('QB', 1, 1024, 512),
-    ('O', 2, 0, 512, 'S'),
-    ('O', 2, 512, 512, 'S'),
-    ('O', 3, 0, 512, 'S'),
-    ('O', 3, 512, 512, 'S'),
-    ('WA', 768, 128, 'S'),
-    ('IA', 512, 128, 'V'),
-    ('QA', 512, 128),
-    ('G', 4),
-    ('QG', 4),
-    ('O', 0, 1024, 512, 'S'),
-    ('O', 1, 1024, 512, 'S'),
-    ('O', 2, 1024, 512, 'S'),
-    ('O', 3, 1024, 512, 'S'),
-    ('WA', 896, 128, 'S'),
-    ('IA', 640, 128, 'V'),
-    ('QA', 640, 128),
-    ('G', 5),
-    ('QG', 5),
-    ('O', 4, 0, 512, 'S'),
-    ('O', 4, 512, 512, 'S'),
-    ('O', 4, 1024, 512, 'S'),
-    ('WA', 1024, 128, 'S'),
-    ('IA', 768, 128, 'V'),
-    ('QA', 768, 128),
-    ('G', 6),
-    ('QG', 6),
-    ('O', 5, 0, 512, 'S'),
-    ('O', 5, 512, 512, 'S'),
-    ('O', 5, 1024, 512, 'S'),
-    ('WA', 1152, 128, 'S'),
-    ('IA', 896, 128, 'V'),
-    ('QA', 896, 128),
-    ('G', 7),
-    ('QG', 7),
-    ('O', 6, 0, 512, 'S'),
-    ('O', 6, 512, 512, 'S'),
-    ('O', 6, 1024, 512, 'S'),
-    ('WA', 1280, 128, 'S'),
-    ('IA', 1024, 128, 'V'),
-    ('QA', 1024, 128),
-    ('G', 8),
-    ('QG', 8),
-    ('O', 7, 512, 512, 'S'),
-    ('O', 7, 0, 512, 'S'),
-    ('O', 7, 1024, 512, 'S'),
-    ('WA', 1408, 128, 'S'),
-    ('IA', 1152, 128, 'V'),
-    ('QA', 1152, 128),
-    ('G', 9),
-    ('QG', 9),
-    ('O', 8, 1024, 512, 'S'),
-    ('O', 8, 0, 512, 'S'),
-    ('O', 8, 512, 512, 'S'),
-    ('IA', 1280, 128, 'V'),
-    ('QA', 1280, 128),
-    ('G', 10),
-    ('QG', 10),
-    ('O', 9, 1024, 512, 'S'),
-    ('O', 9, 0, 512, 'S'),
-    ('O', 9, 512, 512, 'S'),
-    ('IA', 1408, 128, 'V'),
-    ('QA', 1408, 128),
-    ('G', 11),
-    ('QG', 11),
-    ('O', 10, 1024, 512, 'S'),
-    ('O', 10, 0, 512, 'S'),
-    ('O', 10, 512, 512, 'S'),
-    ('O', 11, 1024, 512, 'S'),
-    ('O', 11, 0, 512, 'S'),
-    ('O', 11, 512, 256, 'V'),
-    ('O', 11, 768, 256, 'S'),
+    ('widen_a', 0, 0, 'V'),
+    ('widen_a', 0, 1, 'S'),
+    ('widen_a', 0, 2, 'V'),
+    ('widen_a', 0, 3, 'S'),
+    ('v_column',),
+    ('inter_a', 0, 'V'),
+    ('inter_f', 0, 'V'),
+    ('quant_a', 0),
+    ('quant_f', 0),
+    ('inter_f', 1, 'V'),
+    ('quant_f', 1),
+    ('g_product', 0, 0, 0),
+    ('g_planes', 0, 0, 0, 'S'),
+    ('g_product', 0, 0, 1),
+    ('g_planes', 0, 0, 1, 'S'),
+    ('g_product', 0, 1, 0),
+    ('g_planes', 0, 1, 0, 'S'),
+    ('g_product', 0, 1, 1),
+    ('g_planes', 0, 1, 1, 'S'),
+    ('inter_g', 0),
+    ('quant_g', 0),
+    ('widen_b', 0, 0, 0, 'S'),
+    ('widen_b', 0, 0, 1, 'S'),
+    ('widen_b', 0, 0, 2, 'S'),
+    ('widen_b', 0, 0, 3, 'S'),
+    ('widen_b', 0, 1, 0, 'S'),
+    ('widen_b', 0, 1, 1, 'S'),
+    ('widen_b', 0, 1, 2, 'S'),
+    ('widen_b', 0, 1, 3, 'S'),
+    ('widen_b', 512, 0, 0, 'S'),
+    ('widen_b', 512, 0, 1, 'S'),
+    ('widen_b', 512, 0, 2, 'S'),
+    ('widen_b', 512, 0, 3, 'S'),
+    ('widen_b', 512, 1, 0, 'S'),
+    ('widen_b', 512, 1, 1, 'S'),
+    ('widen_b', 512, 1, 2, 'S'),
+    ('widen_b', 512, 1, 3, 'S'),
+    ('widen_a', 256, 0, 'S'),
+    ('widen_a', 256, 1, 'S'),
+    ('widen_a', 256, 2, 'S'),
+    ('widen_a', 256, 3, 'S'),
+    ('widen_b', 1024, 0, 0, 'S'),
+    ('widen_b', 1024, 0, 1, 'S'),
+    ('widen_b', 1024, 0, 2, 'S'),
+    ('widen_b', 1024, 0, 3, 'S'),
+    ('widen_b', 1024, 1, 0, 'S'),
+    ('widen_b', 1024, 1, 1, 'S'),
+    ('widen_b', 1024, 1, 2, 'S'),
+    ('widen_b', 1024, 1, 3, 'S'),
+    ('inter_b', 0),
+    ('quant_b', 0),
+    ('widen_a', 512, 0, 'S'),
+    ('widen_a', 512, 1, 'S'),
+    ('widen_a', 512, 2, 'S'),
+    ('widen_a', 512, 3, 'S'),
+    ('inter_b', 512),
+    ('quant_b', 512),
+    ('d_columns',),
+    ('out_product', 0, 0),
+    ('out_copy', 0, 0, 'S'),
+    ('add_d', 0, 0),
+    ('store', 0, 0),
+    ('out_product', 1, 0),
+    ('out_copy', 1, 0, 'S'),
+    ('add_d', 1, 0),
+    ('store', 1, 0),
+    ('widen_a', 640, 0, 'S'),
+    ('widen_a', 640, 1, 'S'),
+    ('widen_a', 640, 2, 'S'),
+    ('widen_a', 640, 3, 'S'),
+    ('inter_a', 256, 'V'),
+    ('quant_a', 256),
+    ('g_product', 256, 0, 0),
+    ('g_direct', 256, 0, 0),
+    ('g_product', 256, 0, 1),
+    ('g_direct', 256, 0, 1),
+    ('g_product', 256, 1, 0),
+    ('g_direct', 256, 1, 0),
+    ('g_product', 256, 1, 1),
+    ('g_direct', 256, 1, 1),
+    ('quant_g', 256),
+    ('out_product', 0, 512),
+    ('out_copy', 0, 512, 'S'),
+    ('store', 0, 512),
+    ('out_product', 1, 512),
+    ('out_copy', 1, 512, 'S'),
+    ('store', 1, 512),
+    ('widen_a', 768, 0, 'S'),
+    ('widen_a', 768, 1, 'S'),
+    ('widen_a', 768, 2, 'S'),
+    ('widen_a', 768, 3, 'S'),
+    ('inter_b', 1024),
+    ('quant_b', 1024),
+    ('out_product', 2, 0),
+    ('out_copy', 2, 0, 'S'),
+    ('add_d', 2, 0),
+    ('store', 2, 0),
+    ('out_product', 2, 512),
+    ('out_copy', 2, 512, 'S'),
+    ('store', 2, 512),
+    ('out_product', 3, 0),
+    ('out_copy', 3, 0, 'S'),
+    ('add_d', 3, 0),
+    ('store', 3, 0),
+    ('out_product', 3, 512),
+    ('out_copy', 3, 512, 'S'),
+    ('store', 3, 512),
+    ('widen_a', 896, 0, 'S'),
+    ('widen_a', 896, 1, 'S'),
+    ('widen_a', 896, 2, 'S'),
+    ('widen_a', 896, 3, 'S'),
+    ('inter_a', 512, 'V'),
+    ('quant_a', 512),
+    ('g_product', 512, 0, 0),
+    ('g_direct', 512, 0, 0),
+    ('g_product', 512, 1, 0),
+    ('g_direct', 512, 1, 0),
+    ('quant_g', 512),
+    ('out_product', 0, 1024),
+    ('out_copy', 0, 1024, 'S'),
+    ('store', 0, 1024),
+    ('out_product', 1, 1024),
+    ('out_copy', 1, 1024, 'S'),
+    ('store', 1, 1024),
+    ('out_product', 2, 1024),
+    ('out_copy', 2, 1024, 'S'),
+    ('store', 2, 1024),
+    ('out_product', 3, 1024),
+    ('out_copy', 3, 1024, 'S'),
+    ('store', 3, 1024),
+    ('widen_a', 1024, 0, 'S'),
+    ('widen_a', 1024, 1, 'S'),
+    ('widen_a', 1024, 2, 'S'),
+    ('widen_a', 1024, 3, 'S'),
+    ('inter_a', 640, 'V'),
+    ('quant_a', 640),
+    ('g_product', 640, 0, 0),
+    ('g_direct', 640, 0, 0),
+    ('g_product', 640, 1, 0),
+    ('g_direct', 640, 1, 0),
+    ('quant_g', 640),
+    ('out_product', 4, 0),
+    ('out_copy', 4, 0, 'S'),
+    ('store', 4, 0),
+    ('out_product', 4, 512),
+    ('out_copy', 4, 512, 'S'),
+    ('add_d', 4, 512),
+    ('store', 4, 512),
+    ('out_product', 4, 1024),
+    ('out_copy', 4, 1024, 'S'),
+    ('store', 4, 1024),
+    ('widen_a', 1152, 0, 'S'),
+    ('widen_a', 1152, 1, 'S'),
+    ('widen_a', 1152, 2, 'S'),
+    ('widen_a', 1152, 3, 'S'),
+    ('inter_a', 768, 'V'),
+    ('quant_a', 768),
+    ('g_product', 768, 0, 0),
+    ('g_direct', 768, 0, 0),
+    ('g_product', 768, 1, 0),
+    ('g_direct', 768, 1, 0),
+    ('quant_g', 768),
+    ('out_product', 5, 0),
+    ('out_copy', 5, 0, 'S'),
+    ('store', 5, 0),
+    ('out_product', 5, 512),
+    ('out_copy', 5, 512, 'S'),
+    ('add_d', 5, 512),
+    ('store', 5, 512),
+    ('out_product', 5, 1024),
+    ('out_copy', 5, 1024, 'S'),
+    ('store', 5, 1024),
+    ('widen_a', 1280, 0, 'S'),
+    ('widen_a', 1280, 1, 'S'),
+    ('widen_a', 1280, 2, 'S'),
+    ('widen_a', 1280, 3, 'S'),
+    ('inter_a', 896, 'V'),
+    ('quant_a', 896),
+    ('g_product', 896, 0, 0),
+    ('g_direct', 896, 0, 0),
+    ('g_product', 896, 1, 0),
+    ('g_direct', 896, 1, 0),
+    ('quant_g', 896),
+    ('out_product', 6, 512),
+    ('out_copy', 6, 512, 'S'),
+    ('add_d', 6, 512),
+    ('out_product', 6, 0),
+    ('out_copy', 6, 0, 'S'),
+    ('out_product', 6, 1024),
+    ('out_copy', 6, 1024, 'S'),
+    ('store_rows', 6),
+    ('widen_a', 1408, 0, 'S'),
+    ('widen_a', 1408, 1, 'S'),
+    ('widen_a', 1408, 2, 'S'),
+    ('widen_a', 1408, 3, 'S'),
+    ('inter_a', 1024, 'V'),
+    ('quant_a', 1024),
+    ('g_product', 1024, 0, 0),
+    ('g_direct', 1024, 0, 0),
+    ('g_product', 1024, 1, 0),
+    ('g_direct', 1024, 1, 0),
+    ('quant_g', 1024),
+    ('out_product', 7, 512),
+    ('out_copy', 7, 512, 'S'),
+    ('add_d', 7, 512),
+    ('out_product', 7, 0),
+    ('out_copy', 7, 0, 'S'),
+    ('out_product', 7, 1024),
+    ('out_copy', 7, 1024, 'S'),
+    ('store_rows', 7),
+    ('inter_a', 1152, 'V'),
+    ('quant_a', 1152),
+    ('g_product', 1152, 0, 0),
+    ('g_direct', 1152, 0, 0),
+    ('g_product', 1152, 1, 0),
+    ('g_direct', 1152, 1, 0),
+    ('quant_g', 1152),
+    ('out_product', 8, 1024),
+    ('out_copy', 8, 1024, 'S'),
+    ('add_d', 8, 1024),
+    ('out_product', 8, 0),
+    ('out_copy', 8, 0, 'S'),
+    ('out_product', 8, 512),
+    ('out_copy', 8, 512, 'S'),
+    ('store_rows', 8),
+    ('inter_a', 1280, 'V'),
+    ('quant_a', 1280),
+    ('g_product', 1280, 0, 0),
+    ('g_direct', 1280, 0, 0),
+    ('g_product', 1280, 1, 0),
+    ('g_direct', 1280, 1, 0),
+    ('quant_g', 1280),
+    ('out_product', 9, 1024),
+    ('out_copy', 9, 1024, 'S'),
+    ('add_d', 9, 1024),
+    ('out_product', 9, 0),
+    ('out_copy', 9, 0, 'S'),
+    ('out_product', 9, 512),
+    ('out_copy', 9, 512, 'S'),
+    ('store_rows', 9),
+    ('inter_a', 1408, 'V'),
+    ('quant_a', 1408),
+    ('g_product', 1408, 0, 0),
+    ('g_direct', 1408, 0, 0),
+    ('g_product', 1408, 1, 0),
+    ('g_direct', 1408, 1, 0),
+    ('quant_g', 1408),
+    ('out_product', 10, 1024),
+    ('out_copy', 10, 1024, 'S'),
+    ('add_d', 10, 1024),
+    ('out_product', 10, 0),
+    ('out_copy', 10, 0, 'S'),
+    ('out_product', 10, 512),
+    ('out_copy', 10, 512, 'S'),
+    ('store_rows', 10),
+    ('out_product', 11, 1024),
+    ('out_copy', 11, 1024, 'S'),
+    ('add_d', 11, 1024),
+    ('store', 11, 1024),
+    ('out_product', 11, 0),
+    ('out_copy', 11, 0, 'S'),
+    ('store', 11, 0),
+    ('out_product', 11, 512),
+    ('out_copy', 11, 512, 'S'),
+    ('store', 11, 512),
 ]
 
 
@@ -150,206 +303,223 @@ def tile_listing_cross_covariance_d5_kernel(
     nc = tc.nc
     with ExitStack() as ctx:
         keep = ctx.enter_context(tc.tile_pool(name="keep", bufs=1))
-        work = ctx.enter_context(tc.tile_pool(name="work", bufs=4))
-        outs = ctx.enter_context(tc.tile_pool(name="outs", bufs=12))
-        ps = ctx.enter_context(tc.psum_pool(name="ps", bufs=4))
+        work = ctx.enter_context(tc.tile_pool(name="work", bufs=2))
+        outs = ctx.enter_context(tc.tile_pool(name="outs", bufs=8))
+        psum = ctx.enter_context(tc.psum_pool(name="psum", bufs=4))
 
         a_by = keep.tile([P, T, N], U8, name="a_by", align_bytes=64)
-        b_by = keep.tile([P, PASSES, T, N], U8, name="b_by", align_bytes=64)
+        b_by = keep.tile([P, G, T, N], U8, name="b_by", align_bytes=64)
         f_raw = keep.tile([P, T, J], BF16, name="f_raw", align_bytes=64)
         a_sc = keep.tile([P, T], F32, name="a_sc")
-        b_sc = keep.tile([P, PASSES, T], F32, name="b_sc")
-        v_sb = keep.tile([P, PASSES, T], BF16, name="v_sb")
-        d_rows = keep.tile([P, P], BF16, name="d_rows")
+        b_sc = keep.tile([P, G, T], F32, name="b_sc")
+        v_row = keep.tile([P, G, T], BF16, name="v_row")
+        v_col = keep.tile([P, G, T], F32, name="v_col")
+        d_row = keep.tile([P, P], BF16, name="d_row")
         d_col = keep.tile([P, MT], F32, name="d_col")
         ident = keep.tile([P, P], BF16, name="ident")
 
-        a_cod = keep.tile([P, N], U32, name="a_cod", align_bytes=64)
-        a_qs = keep.tile([P, N], U8, name="a_qs", align_bytes=64)
-        f_cod = keep.tile([P, J], U32, name="f_cod", align_bytes=64)
-        f_qs = keep.tile([P, J], U8, name="f_qs", align_bytes=64)
-        b_cod = keep.tile([P, PASSES, N], U32, name="b_cod", align_bytes=64)
-        b_qs = keep.tile([P, PASSES, N], U8, name="b_qs", align_bytes=64)
-        g_cod = keep.tile([P, MT, PASSES * P], U32, name="g_cod", align_bytes=64)
-        g_qs = keep.tile([P, MT, PASSES * P], U8, name="g_qs", align_bytes=64)
+        def operand(name, width):
+            codes = keep.tile([P, width], U32, name=name + "_codes", align_bytes=64)
+            scales = keep.tile([P, width], U8, name=name + "_scales", align_bytes=64)
+            return codes, scales
+
+        f_q = [operand("f%d" % g, BANK) for g in range(G)]
+        a_q = {c: operand("a%d" % c, w) for c, w in A_CHUNKS}
+        g_q = {c: operand("g%d" % c, G * w) for c, w in A_CHUNKS}
+        b_q = {c: operand("b%d" % c, G * w) for c, w in B_CHUNKS}
+        width_a = dict(A_CHUNKS)
+        width_b = dict(B_CHUNKS)
 
         a_hbm = A_bytes.rearrange("(p t) n -> p t n", t=T)
         b_hbm = B_bytes.rearrange("(g p t) n -> g p t n", p=P, t=T)
         f_hbm = F.rearrange("(p t) j -> p t j", t=T)
-        nc.sync.dma_start(out=a_sc[:], in_=A_scale.rearrange("(p t) o -> p (t o)", t=T))
-        nc.sync.dma_start(out=a_by[:, :, 0:CH], in_=a_hbm[:, :, 0:CH])
-        nc.sync.dma_start(out=f_raw[:, :, 0:CH], in_=f_hbm[:, :, 0:CH])
-        nc.sync.dma_start(out=f_raw[:, :, CH:J], in_=f_hbm[:, :, CH:J])
-        nc.sync.dma_start(out=b_sc[:], in_=B_scale.rearrange("(g p t) o -> p g (t o)", p=P, t=T))
-        nc.sync.dma_start(out=v_sb[:], in_=v.rearrange("(g p t) -> p g t", p=P, t=T))
-        for g in range(PASSES):
-            for h in range(2):
-                nc.sync.dma_start(
-                    out=b_by[:, g, 2 * h : 2 * h + 2, :], in_=b_hbm[g, :, 2 * h : 2 * h + 2, :]
-                )
-        nc.sync.dma_start(out=a_by[:, :, CH:N], in_=a_hbm[:, :, CH:N])
-        nc.vector.memset(d_rows[:], 0.0)
+        load = nc.sync.dma_start
+        load(out=a_sc[:], in_=A_scale.rearrange("(p t) o -> p (t o)", t=T))
+        load(out=a_by[:, :, 0:HALF], in_=a_hbm[:, :, 0:HALF])
+        load(out=v_row[:], in_=v.rearrange("(g p t) -> p g t", p=P, t=T))
+        for g in range(G):
+            cols = slice(g * BANK, (g + 1) * BANK)
+            load(out=f_raw[:, :, cols], in_=f_hbm[:, :, cols])
+        load(out=b_sc[:], in_=B_scale.rearrange("(g p t) o -> p g (t o)", p=P, t=T))
+        for g in range(G):
+            for t in range(0, T, 2):
+                load(out=b_by[:, g, t : t + 2, :], in_=b_hbm[g, :, t : t + 2, :])
+        load(out=a_by[:, :, HALF:N], in_=a_hbm[:, :, HALF:N])
+        nc.vector.memset(d_row[:], 0.0)
         make_identity(nc, ident[:])
-        nc.gpsimd.dma_start(out=d_rows[0:MT, :], in_=d.rearrange("(c p) -> c p", p=P))
+        load(out=d_row[0:MT, :], in_=d.rearrange("(c p) -> c p", p=P))
 
-        planes = {}
-        mixed = {}
+        tiles = {}
 
-        def widen(key, src, scale, w, eng):
-            pl = work.tile([P, T, w], BF16, name="pl" + str(w), bufs=NPL, align_bytes=64)
-            planes[key] = pl
-            for t in range(T):
-                if eng == "S" or (eng == "M" and t % 2):
-                    nc.scalar.activation(
-                        out=pl[:, t, :], in_=src[:, t, :].bitcast(E4M3), func=COPY, scale=scale[:, t : t + 1]
-                    )
-                else:
-                    nc.vector.tensor_scalar(
-                        out=pl[:, t, :], in0=src[:, t, :].bitcast(E4M3), scalar1=scale[:, t : t + 1], scalar2=None, op0=MULT
-                    )
+        def get(key, shape, name, bufs):
+            if key not in tiles:
+                tiles[key] = work.tile(shape, BF16, name=name, bufs=bufs, align_bytes=64)
+            return tiles[key]
 
-        def inter(key, w, eng):
-            x = work.tile([P, T * w], BF16, name="ix" + str(w), align_bytes=64)
-            mixed[key] = x
-            o = x[:].rearrange("p (c i t) -> p c t i", i=4, t=T)
-            i = planes[key][:].rearrange("p t (c i) -> p c t i", i=4)
-            if eng == "S":
-                nc.scalar.copy(out=o, in_=i)
+        def get_mixed(key, width):
+            return get(key, [P, width], "mixed%d" % width, 4 if width < 2048 else 3)
+
+        def times_column(engine, out, in_, column):
+            if engine == "S":
+                nc.scalar.activation(out=out, in_=in_, func=COPY, scale=column)
             else:
-                nc.vector.tensor_copy(out=o, in_=i)
+                nc.vector.tensor_scalar(out=out, in0=in_, scalar1=column, scalar2=None, op0=MULT)
 
-        def pe_inter(key, w, eng):
-            x = work.tile([P, T * w], BF16, name="ix" + str(w), align_bytes=64)
-            mixed[key] = x
-            pl = planes[key]
-            for h in range(w // 256):
-                bank = ps.tile([P, 2 * CH], BF16, name="gb")
-                for q in range(2):
-                    n0 = h * 256 + q * P
-                    nc.tensor.matmul(
-                        out=bank[:, q * CH : (q + 1) * CH],
-                        lhsT=ident[:],
-                        rhs=pl[:, :, n0 : n0 + P].rearrange("p t n -> p n t"),
-                        start=True,
-                        stop=True,
-                    )
-                o = x[:, h * 2 * CH : (h + 1) * 2 * CH]
-                e = eng[h % len(eng)]
-                if e == "S":
-                    nc.scalar.copy(out=o, in_=bank[:])
-                else:
-                    nc.vector.tensor_copy(out=o, in_=bank[:])
+        def widen_a(c, t, engine):
+            w = width_a[c]
+            planes = get(("pa", c), [P, T, w], "a_planes%d" % w, 4)
+            times_column(engine, planes[:, t, :], a_by[:, t, c : c + w].bitcast(E4M3), a_sc[:, t : t + 1])
 
-        def quant(cod, qs, src):
-            nc.vector.quantize_mx(out=cod.bitcast(FP8X4), scales=qs, in_=src[:])
+        def widen_b(c, g, t, engine):
+            w = width_b[c]
+            planes = get(("pb", c), [P, T, G * w], "b_planes%d" % w, 3)
+            times_column(
+                engine, planes[:, t, g * w : (g + 1) * w], b_by[:, g, t, c : c + w].bitcast(E4M3), b_sc[:, g, t : t + 1]
+            )
 
-        def f_inter(g, eng):
-            x = work.tile([P, T * CH], BF16, name="fx", bufs=2, align_bytes=64)
-            mixed["F", g] = x
-            o = x[:].rearrange("p (t m j) -> p t m j", t=T, j=T)
-            i = f_raw[:, :, g * CH : (g + 1) * CH].rearrange("p j (m t) -> p t m j", t=T)
-            if eng == "S":
-                nc.scalar.copy(out=o, in_=i)
-            else:
-                nc.vector.tensor_copy(out=o, in_=i)
+        def interleave(planes, w, key, name, engine="V"):
+            mixed = get_mixed(key, T * w)
+            copy = nc.scalar.copy if engine == "S" else nc.vector.tensor_copy
+            copy(
+                out=mixed[:].rearrange("p (c i t) -> p c t i", i=4, t=T),
+                in_=planes[:].rearrange("p t (c i) -> p c t i", i=4),
+            )
 
-        gx = {}
+        def quantize(operand, mixed):
+            codes, scales = operand
+            nc.vector.quantize_mx(out=codes[:].bitcast(FP8X4), scales=scales[:], in_=mixed[:])
 
-        def g_mm(mt):
-            x = work.tile([P, PASSES * T * P], BF16, name="gx", align_bytes=64)
-            gx[mt] = x
-            i0 = mt * P
-            for g in range(PASSES):
-                bank = ps.tile([P, T, P], F32, name="gb")
+        def inter_a(c, engine):
+            interleave(tiles["pa", c], width_a[c], ("xa", c), "a_mixed", engine)
+
+        def quant_a(c):
+            quantize(a_q[c], tiles["xa", c])
+
+        def inter_b(c):
+            interleave(tiles["pb", c], G * width_b[c], ("xb", c), "b_mixed")
+
+        def quant_b(c):
+            quantize(b_q[c], tiles["xb", c])
+
+        def inter_f(g, engine):
+            mixed = get_mixed(("xf", g), T * BANK)
+            copy = nc.scalar.copy if engine == "S" else nc.vector.tensor_copy
+            copy(
+                out=mixed[:].rearrange("p (t m j) -> p t m j", t=T, j=T),
+                in_=f_raw[:, :, g * BANK : (g + 1) * BANK].rearrange("p j (m t) -> p t m j", t=T),
+            )
+
+        def quant_f(g):
+            quantize(f_q[g], tiles["xf", g])
+
+        def multiply(bank, left, l0, right, r0, w, first=True, last=True):
+            nc.tensor.matmul_mx(
+                out=bank,
+                lhsT=left[0][:, l0 : l0 + P].bitcast(FP8X4),
+                lhsT_scale=left[1][:, l0 : l0 + P],
+                rhs=right[0][:, r0 : r0 + w].bitcast(FP8X4),
+                rhs_scale=right[1][:, r0 : r0 + w],
+                start=first,
+                stop=last,
+            )
+
+        def g_product(c, g, b):
+            w = width_a[c]
+            if c in TWO_INPUT:
+                bank = psum.tile([P, T, P], F32, name="g_bank")
                 for t in range(T):
-                    j0 = (g * T + t) * P
-                    nc.tensor.matmul_mx(
-                        out=bank[:, t, :],
-                        lhsT=f_cod[:, j0 : j0 + P].bitcast(FP8X4),
-                        lhsT_scale=f_qs[:, j0 : j0 + P],
-                        rhs=a_cod[:, i0 : i0 + P].bitcast(FP8X4),
-                        rhs_scale=a_qs[:, i0 : i0 + P],
-                        start=True,
-                        stop=True,
-                    )
-                nc.vector.tensor_tensor(
-                    out=x[:, g * CH : (g + 1) * CH].rearrange("p (c i t) -> p c t i", i=4, t=T),
-                    in0=bank[:].rearrange("p t (c i) -> p c t i", i=4),
-                    in1=v_sb[:, g : g + 1, :].unsqueeze(3).to_broadcast([P, P // 4, T, 4]),
-                    op=MULT,
-                )
-
-        def g_q(mt):
-            quant(g_cod[:, mt, :], g_qs[:, mt, :], gx[mt])
-
-        def out_mm(mt, c0, w, eng):
-            bank = ps.tile([P, CH], F32, name="ob")
-            for g in range(PASSES):
-                nc.tensor.matmul_mx(
-                    out=bank[:, 0:w],
-                    lhsT=g_cod[:, mt, g * P : (g + 1) * P].bitcast(FP8X4),
-                    lhsT_scale=g_qs[:, mt, g * P : (g + 1) * P],
-                    rhs=b_cod[:, g, c0 : c0 + w].bitcast(FP8X4),
-                    rhs_scale=b_qs[:, g, c0 : c0 + w],
-                    start=(g == 0),
-                    stop=(g == PASSES - 1),
-                )
-            o = outs.tile([P, w], F32, name="o" + str(w))
-            if eng == "S":
-                nc.scalar.copy(out=o[:], in_=bank[:, 0:w])
+                    multiply(bank[:, t, :], f_q[g], t * P, a_q[c], b * P, P)
             else:
-                nc.vector.tensor_copy(out=o[:], in_=bank[:, 0:w])
-            x0 = mt * P - c0
-            if 0 <= x0 < w:
-                nc.vector.scalar_tensor_tensor(
-                    out=o[:, x0 : x0 + P],
-                    in0=ident[:],
-                    scalar=d_col[:, mt : mt + 1],
-                    in1=o[:, x0 : x0 + P],
-                    op0=MULT,
-                    op1=ADD,
-                )
-            nc.sync.dma_start(out=out[mt * P : (mt + 1) * P, c0 : c0 + w], in_=o[:])
+                bank = psum.tile([P, BANK // w, w], F32, name="g_bank")
+                for q in range(BANK // w):
+                    multiply(bank[:, q, :], f_q[g], (b * (BANK // w) + q) * P, a_q[c], 0, w)
+            tiles["gb", c, g, b] = bank
 
-        def d_setup():
-            dp = ps.tile([P, P], BF16, name="gb")
-            nc.tensor.transpose(dp[:], d_rows[:], ident[:])
-            nc.vector.tensor_copy(out=d_col[:], in_=dp[:, 0:MT])
+        def g_planes(c, g, b, engine):
+            w = width_a[c]
+            planes = get(("pg", c), [P, T, G * w], "g_planes%d" % w, 2)
+            bank = tiles["gb", c, g, b]
+            for q in range(BANK // w):
+                t = b * (BANK // w) + q
+                times_column(engine, planes[:, t, g * w : (g + 1) * w], bank[:, q, :], v_col[:, g, t : t + 1])
 
-        def run():
-            for s in SEQ:
-                k = s[0]
-                if k == "WA":
-                    widen(("A", s[1]), a_by[:, :, s[1] : s[1] + s[2]], a_sc, s[2], s[3])
-                elif k == "WB":
-                    widen(("B", s[1], s[2]), b_by[:, s[1], :, s[2] : s[2] + s[3]], b_sc[:, s[1], :], s[3], s[4])
-                elif k == "IA":
-                    inter(("A", s[1]), s[2], s[3])
-                elif k == "IB":
-                    inter(("B", s[1], s[2]), s[3], s[4])
-                elif k == "PB":
-                    pe_inter(("B", s[1], s[2]), s[3], s[4])
-                elif k == "PA":
-                    pe_inter(("A", s[1]), s[2], s[3])
-                elif k == "QA":
-                    quant(a_cod[:, s[1] : s[1] + s[2]], a_qs[:, s[1] : s[1] + s[2]], mixed["A", s[1]])
-                elif k == "QB":
-                    quant(b_cod[:, s[1], s[2] : s[2] + s[3]], b_qs[:, s[1], s[2] : s[2] + s[3]], mixed["B", s[1], s[2]])
-                elif k == "IF":
-                    f_inter(s[1], s[2])
-                elif k == "QF":
-                    quant(f_cod[:, s[1] * CH : (s[1] + 1) * CH], f_qs[:, s[1] * CH : (s[1] + 1) * CH], mixed["F", s[1]])
-                elif k == "G":
-                    g_mm(s[1])
-                elif k == "QG":
-                    g_q(s[1])
-                elif k == "D":
-                    d_setup()
-                elif k == "O":
-                    out_mm(s[1], s[2], s[3], s[4])
+        def g_direct(c, g, b):
+            w = width_a[c]
+            mixed = get_mixed(("xg", c), T * G * w)
+            x0 = T * (g * w + b * P)
+            nc.vector.tensor_tensor(
+                out=mixed[:, x0 : x0 + T * P].rearrange("p (c i t) -> p c t i", i=4, t=T),
+                in0=tiles["gb", c, g, b][:].rearrange("p t (c i) -> p c t i", i=4),
+                in1=v_row[:, g : g + 1, :].unsqueeze(3).to_broadcast([P, P // 4, T, 4]),
+                op=MULT,
+            )
 
+        def inter_g(c):
+            w = width_a[c]
+            mixed = get_mixed(("xg", c), T * G * w)
+            planes = tiles["pg", c]
+            nc.vector.tensor_copy(
+                out=mixed[:].rearrange("p (c i t) -> p c t i", i=4, t=T),
+                in_=planes[:].rearrange("p t (c i) -> p c t i", i=4),
+            )
+
+        def quant_g(c):
+            quantize(g_q[c], tiles["xg", c])
+
+        def out_product(m, c):
+            ca = max(a for a in width_a if a <= m * P)
+            w = width_b[c]
+            bank = psum.tile([P, BANK], F32, name="out_bank")
+            for g in range(G):
+                multiply(bank[:, 0:w], g_q[ca], g * width_a[ca] + m * P - ca, b_q[c], g * w, w, g == 0, g == G - 1)
+            tiles["ob", m, c] = bank
+
+        def out_block(m, c):
+            w = width_b[c]
+            if m < WHOLE_ROWS_FROM:
+                if ("o", m, c) not in tiles:
+                    block = outs.tile([P, w], F32, name="o%d" % w)
+                    tiles["o", m, c] = block
+                return tiles["o", m, c][:]
+            if ("o", m) not in tiles:
+                rows = outs.tile([P, N], F32, name="o_rows", bufs=6)
+                tiles["o", m] = rows
+            return tiles["o", m][:, c : c + w]
+
+        def out_copy(m, c, engine):
+            copy = nc.scalar.copy if engine == "S" else nc.vector.tensor_copy
+            copy(out=out_block(m, c), in_=tiles["ob", m, c][:, 0 : width_b[c]])
+
+        def add_d(m, c):
+            block = out_block(m, c)[:, m * P - c : (m + 1) * P - c]
+            nc.vector.scalar_tensor_tensor(
+                out=block, in0=ident[:], scalar=d_col[:, m : m + 1], in1=block, op0=MULT, op1=ADD
+            )
+
+        def store(m, c):
+            nc.sync.dma_start(out=out[m * P : (m + 1) * P, c : c + width_b[c]], in_=out_block(m, c))
+
+        def store_rows(m):
+            nc.sync.dma_start(out=out[m * P : (m + 1) * P, :], in_=tiles["o", m][:])
+
+        def v_column():
+            nc.vector.tensor_copy(out=v_col[:], in_=v_row[:])
+
+        def d_columns():
+            turned = psum.tile([P, P], BF16, name="out_bank")
+            nc.tensor.transpose(turned[:], d_row[:], ident[:])
+            nc.vector.tensor_copy(out=d_col[:], in_=turned[:, 0:MT])
+
+        actions = {
+            "widen_a": widen_a, "widen_b": widen_b, "inter_a": inter_a, "quant_a": quant_a, "inter_b": inter_b,
+            "quant_b": quant_b, "inter_f": inter_f, "quant_f": quant_f, "g_product": g_product, "g_planes": g_planes,
+            "g_direct": g_direct, "inter_g": inter_g, "quant_g": quant_g, "out_product": out_product,
+            "out_copy": out_copy, "add_d": add_d, "store": store, "store_rows": store_rows, "v_column": v_column, "d_columns": d_columns,
+        }
         if MANUAL:
             with tc.manual_schedule():
-                run()
+                for step in SEQ:
+                    actions[step[0]](*step[1:])
         else:
-            run()
+            for step in SEQ:
+                actions[step[0]](*step[1:])

from contextlib import ExitStack

import concourse.mybir as mybir
from concourse.masks import make_identity

N, K, J = 1536, 512, 1024
FLOPS = 2 * (N * K * J + N * J * N)

F32 = mybir.dt.float32
BF16 = mybir.dt.bfloat16
U32 = mybir.dt.uint32
U8 = mybir.dt.uint8
E4M3 = mybir.dt.float8_e4m3fn
FP8X4 = mybir.dt.float8_e4m3fn_x4
MULT = mybir.AluOpType.mult
ADD = mybir.AluOpType.add
COPY = mybir.ActivationFunctionType.Copy

P = 128
T = 4
G = J // (P * T)
MT = N // P
BANK = 512
HALF = N // 2
WHOLE_ROWS_FROM = 6

MANUAL = False
A_CHUNKS = [(0, 256), (256, 256), (512, 128), (640, 128), (768, 128), (896, 128), (1024, 128), (1152, 128), (1280, 128), (1408, 128)]
B_CHUNKS = [(0, 512), (512, 512), (1024, 512)]
TWO_INPUT = [256, 512, 640, 768, 896, 1024, 1152, 1280, 1408]
SEQ = [
    ('widen_a', 0, 0, 'V'),
    ('widen_a', 0, 1, 'S'),
    ('widen_a', 0, 2, 'V'),
    ('widen_a', 0, 3, 'S'),
    ('v_column',),
    ('inter_a', 0, 'V'),
    ('inter_f', 0, 'V'),
    ('quant_a', 0),
    ('quant_f', 0),
    ('inter_f', 1, 'V'),
    ('quant_f', 1),
    ('g_product', 0, 0, 0),
    ('g_planes', 0, 0, 0, 'S'),
    ('g_product', 0, 0, 1),
    ('g_planes', 0, 0, 1, 'S'),
    ('g_product', 0, 1, 0),
    ('g_planes', 0, 1, 0, 'S'),
    ('g_product', 0, 1, 1),
    ('g_planes', 0, 1, 1, 'S'),
    ('inter_g', 0),
    ('quant_g', 0),
    ('widen_b', 0, 0, 0, 'S'),
    ('widen_b', 0, 0, 1, 'S'),
    ('widen_b', 0, 0, 2, 'S'),
    ('widen_b', 0, 0, 3, 'S'),
    ('widen_b', 0, 1, 0, 'S'),
    ('widen_b', 0, 1, 1, 'S'),
    ('widen_b', 0, 1, 2, 'S'),
    ('widen_b', 0, 1, 3, 'S'),
    ('widen_b', 512, 0, 0, 'S'),
    ('widen_b', 512, 0, 1, 'S'),
    ('widen_b', 512, 0, 2, 'S'),
    ('widen_b', 512, 0, 3, 'S'),
    ('widen_b', 512, 1, 0, 'S'),
    ('widen_b', 512, 1, 1, 'S'),
    ('widen_b', 512, 1, 2, 'S'),
    ('widen_b', 512, 1, 3, 'S'),
    ('widen_a', 256, 0, 'S'),
    ('widen_a', 256, 1, 'S'),
    ('widen_a', 256, 2, 'S'),
    ('widen_a', 256, 3, 'S'),
    ('widen_b', 1024, 0, 0, 'S'),
    ('widen_b', 1024, 0, 1, 'S'),
    ('widen_b', 1024, 0, 2, 'S'),
    ('widen_b', 1024, 0, 3, 'S'),
    ('widen_b', 1024, 1, 0, 'S'),
    ('widen_b', 1024, 1, 1, 'S'),
    ('widen_b', 1024, 1, 2, 'S'),
    ('widen_b', 1024, 1, 3, 'S'),
    ('inter_b', 0),
    ('quant_b', 0),
    ('widen_a', 512, 0, 'S'),
    ('widen_a', 512, 1, 'S'),
    ('widen_a', 512, 2, 'S'),
    ('widen_a', 512, 3, 'S'),
    ('inter_b', 512),
    ('quant_b', 512),
    ('d_columns',),
    ('out_product', 0, 0),
    ('out_copy', 0, 0, 'S'),
    ('add_d', 0, 0),
    ('store', 0, 0),
    ('out_product', 1, 0),
    ('out_copy', 1, 0, 'S'),
    ('add_d', 1, 0),
    ('store', 1, 0),
    ('widen_a', 640, 0, 'S'),
    ('widen_a', 640, 1, 'S'),
    ('widen_a', 640, 2, 'S'),
    ('widen_a', 640, 3, 'S'),
    ('inter_a', 256, 'V'),
    ('quant_a', 256),
    ('g_product', 256, 0, 0),
    ('g_direct', 256, 0, 0),
    ('g_product', 256, 0, 1),
    ('g_direct', 256, 0, 1),
    ('g_product', 256, 1, 0),
    ('g_direct', 256, 1, 0),
    ('g_product', 256, 1, 1),
    ('g_direct', 256, 1, 1),
    ('quant_g', 256),
    ('out_product', 0, 512),
    ('out_copy', 0, 512, 'S'),
    ('store', 0, 512),
    ('out_product', 1, 512),
    ('out_copy', 1, 512, 'S'),
    ('store', 1, 512),
    ('widen_a', 768, 0, 'S'),
    ('widen_a', 768, 1, 'S'),
    ('widen_a', 768, 2, 'S'),
    ('widen_a', 768, 3, 'S'),
    ('inter_b', 1024),
    ('quant_b', 1024),
    ('out_product', 2, 0),
    ('out_copy', 2, 0, 'S'),
    ('add_d', 2, 0),
    ('store', 2, 0),
    ('out_product', 2, 512),
    ('out_copy', 2, 512, 'S'),
    ('store', 2, 512),
    ('out_product', 3, 0),
    ('out_copy', 3, 0, 'S'),
    ('add_d', 3, 0),
    ('store', 3, 0),
    ('out_product', 3, 512),
    ('out_copy', 3, 512, 'S'),
    ('store', 3, 512),
    ('widen_a', 896, 0, 'S'),
    ('widen_a', 896, 1, 'S'),
    ('widen_a', 896, 2, 'S'),
    ('widen_a', 896, 3, 'S'),
    ('inter_a', 512, 'V'),
    ('quant_a', 512),
    ('g_product', 512, 0, 0),
    ('g_direct', 512, 0, 0),
    ('g_product', 512, 1, 0),
    ('g_direct', 512, 1, 0),
    ('quant_g', 512),
    ('out_product', 0, 1024),
    ('out_copy', 0, 1024, 'S'),
    ('store', 0, 1024),
    ('out_product', 1, 1024),
    ('out_copy', 1, 1024, 'S'),
    ('store', 1, 1024),
    ('out_product', 2, 1024),
    ('out_copy', 2, 1024, 'S'),
    ('store', 2, 1024),
    ('out_product', 3, 1024),
    ('out_copy', 3, 1024, 'S'),
    ('store', 3, 1024),
    ('widen_a', 1024, 0, 'S'),
    ('widen_a', 1024, 1, 'S'),
    ('widen_a', 1024, 2, 'S'),
    ('widen_a', 1024, 3, 'S'),
    ('inter_a', 640, 'V'),
    ('quant_a', 640),
    ('g_product', 640, 0, 0),
    ('g_direct', 640, 0, 0),
    ('g_product', 640, 1, 0),
    ('g_direct', 640, 1, 0),
    ('quant_g', 640),
    ('out_product', 4, 0),
    ('out_copy', 4, 0, 'S'),
    ('store', 4, 0),
    ('out_product', 4, 512),
    ('out_copy', 4, 512, 'S'),
    ('add_d', 4, 512),
    ('store', 4, 512),
    ('out_product', 4, 1024),
    ('out_copy', 4, 1024, 'S'),
    ('store', 4, 1024),
    ('widen_a', 1152, 0, 'S'),
    ('widen_a', 1152, 1, 'S'),
    ('widen_a', 1152, 2, 'S'),
    ('widen_a', 1152, 3, 'S'),
    ('inter_a', 768, 'V'),
    ('quant_a', 768),
    ('g_product', 768, 0, 0),
    ('g_direct', 768, 0, 0),
    ('g_product', 768, 1, 0),
    ('g_direct', 768, 1, 0),
    ('quant_g', 768),
    ('out_product', 5, 0),
    ('out_copy', 5, 0, 'S'),
    ('store', 5, 0),
    ('out_product', 5, 512),
    ('out_copy', 5, 512, 'S'),
    ('add_d', 5, 512),
    ('store', 5, 512),
    ('out_product', 5, 1024),
    ('out_copy', 5, 1024, 'S'),
    ('store', 5, 1024),
    ('widen_a', 1280, 0, 'S'),
    ('widen_a', 1280, 1, 'S'),
    ('widen_a', 1280, 2, 'S'),
    ('widen_a', 1280, 3, 'S'),
    ('inter_a', 896, 'V'),
    ('quant_a', 896),
    ('g_product', 896, 0, 0),
    ('g_direct', 896, 0, 0),
    ('g_product', 896, 1, 0),
    ('g_direct', 896, 1, 0),
    ('quant_g', 896),
    ('out_product', 6, 512),
    ('out_copy', 6, 512, 'S'),
    ('add_d', 6, 512),
    ('out_product', 6, 0),
    ('out_copy', 6, 0, 'S'),
    ('out_product', 6, 1024),
    ('out_copy', 6, 1024, 'S'),
    ('store_rows', 6),
    ('widen_a', 1408, 0, 'S'),
    ('widen_a', 1408, 1, 'S'),
    ('widen_a', 1408, 2, 'S'),
    ('widen_a', 1408, 3, 'S'),
    ('inter_a', 1024, 'V'),
    ('quant_a', 1024),
    ('g_product', 1024, 0, 0),
    ('g_direct', 1024, 0, 0),
    ('g_product', 1024, 1, 0),
    ('g_direct', 1024, 1, 0),
    ('quant_g', 1024),
    ('out_product', 7, 512),
    ('out_copy', 7, 512, 'S'),
    ('add_d', 7, 512),
    ('out_product', 7, 0),
    ('out_copy', 7, 0, 'S'),
    ('out_product', 7, 1024),
    ('out_copy', 7, 1024, 'S'),
    ('store_rows', 7),
    ('inter_a', 1152, 'V'),
    ('quant_a', 1152),
    ('g_product', 1152, 0, 0),
    ('g_direct', 1152, 0, 0),
    ('g_product', 1152, 1, 0),
    ('g_direct', 1152, 1, 0),
    ('quant_g', 1152),
    ('out_product', 8, 1024),
    ('out_copy', 8, 1024, 'S'),
    ('add_d', 8, 1024),
    ('out_product', 8, 0),
    ('out_copy', 8, 0, 'S'),
    ('out_product', 8, 512),
    ('out_copy', 8, 512, 'S'),
    ('store_rows', 8),
    ('inter_a', 1280, 'V'),
    ('quant_a', 1280),
    ('g_product', 1280, 0, 0),
    ('g_direct', 1280, 0, 0),
    ('g_product', 1280, 1, 0),
    ('g_direct', 1280, 1, 0),
    ('quant_g', 1280),
    ('out_product', 9, 1024),
    ('out_copy', 9, 1024, 'S'),
    ('add_d', 9, 1024),
    ('out_product', 9, 0),
    ('out_copy', 9, 0, 'S'),
    ('out_product', 9, 512),
    ('out_copy', 9, 512, 'S'),
    ('store_rows', 9),
    ('inter_a', 1408, 'V'),
    ('quant_a', 1408),
    ('g_product', 1408, 0, 0),
    ('g_direct', 1408, 0, 0),
    ('g_product', 1408, 1, 0),
    ('g_direct', 1408, 1, 0),
    ('quant_g', 1408),
    ('out_product', 10, 1024),
    ('out_copy', 10, 1024, 'S'),
    ('add_d', 10, 1024),
    ('out_product', 10, 0),
    ('out_copy', 10, 0, 'S'),
    ('out_product', 10, 512),
    ('out_copy', 10, 512, 'S'),
    ('store_rows', 10),
    ('out_product', 11, 1024),
    ('out_copy', 11, 1024, 'S'),
    ('add_d', 11, 1024),
    ('store', 11, 1024),
    ('out_product', 11, 0),
    ('out_copy', 11, 0, 'S'),
    ('store', 11, 0),
    ('out_product', 11, 512),
    ('out_copy', 11, 512, 'S'),
    ('store', 11, 512),
]


def tile_listing_cross_covariance_d5_kernel(
    tc, A_bytes, A_scale, B_bytes, B_scale, F, v, d, out
):
    nc = tc.nc
    with ExitStack() as ctx:
        keep = ctx.enter_context(tc.tile_pool(name="keep", bufs=1))
        work = ctx.enter_context(tc.tile_pool(name="work", bufs=2))
        outs = ctx.enter_context(tc.tile_pool(name="outs", bufs=8))
        psum = ctx.enter_context(tc.psum_pool(name="psum", bufs=4))

        a_by = keep.tile([P, T, N], U8, name="a_by", align_bytes=64)
        b_by = keep.tile([P, G, T, N], U8, name="b_by", align_bytes=64)
        f_raw = keep.tile([P, T, J], BF16, name="f_raw", align_bytes=64)
        a_sc = keep.tile([P, T], F32, name="a_sc")
        b_sc = keep.tile([P, G, T], F32, name="b_sc")
        v_row = keep.tile([P, G, T], BF16, name="v_row")
        v_col = keep.tile([P, G, T], F32, name="v_col")
        d_row = keep.tile([P, P], BF16, name="d_row")
        d_col = keep.tile([P, MT], F32, name="d_col")
        ident = keep.tile([P, P], BF16, name="ident")

        def operand(name, width):
            codes = keep.tile([P, width], U32, name=name + "_codes", align_bytes=64)
            scales = keep.tile([P, width], U8, name=name + "_scales", align_bytes=64)
            return codes, scales

        f_q = [operand("f%d" % g, BANK) for g in range(G)]
        a_q = {c: operand("a%d" % c, w) for c, w in A_CHUNKS}
        g_q = {c: operand("g%d" % c, G * w) for c, w in A_CHUNKS}
        b_q = {c: operand("b%d" % c, G * w) for c, w in B_CHUNKS}
        width_a = dict(A_CHUNKS)
        width_b = dict(B_CHUNKS)

        a_hbm = A_bytes.rearrange("(p t) n -> p t n", t=T)
        b_hbm = B_bytes.rearrange("(g p t) n -> g p t n", p=P, t=T)
        f_hbm = F.rearrange("(p t) j -> p t j", t=T)
        load = nc.sync.dma_start
        load(out=a_sc[:], in_=A_scale.rearrange("(p t) o -> p (t o)", t=T))
        load(out=a_by[:, :, 0:HALF], in_=a_hbm[:, :, 0:HALF])
        load(out=v_row[:], in_=v.rearrange("(g p t) -> p g t", p=P, t=T))
        for g in range(G):
            cols = slice(g * BANK, (g + 1) * BANK)
            load(out=f_raw[:, :, cols], in_=f_hbm[:, :, cols])
        load(out=b_sc[:], in_=B_scale.rearrange("(g p t) o -> p g (t o)", p=P, t=T))
        for g in range(G):
            for t in range(0, T, 2):
                load(out=b_by[:, g, t : t + 2, :], in_=b_hbm[g, :, t : t + 2, :])
        load(out=a_by[:, :, HALF:N], in_=a_hbm[:, :, HALF:N])
        nc.vector.memset(d_row[:], 0.0)
        make_identity(nc, ident[:])
        load(out=d_row[0:MT, :], in_=d.rearrange("(c p) -> c p", p=P))

        tiles = {}

        def get(key, shape, name, bufs):
            if key not in tiles:
                tiles[key] = work.tile(shape, BF16, name=name, bufs=bufs, align_bytes=64)
            return tiles[key]

        def get_mixed(key, width):
            return get(key, [P, width], "mixed%d" % width, 4 if width < 2048 else 3)

        def times_column(engine, out, in_, column):
            if engine == "S":
                nc.scalar.activation(out=out, in_=in_, func=COPY, scale=column)
            else:
                nc.vector.tensor_scalar(out=out, in0=in_, scalar1=column, scalar2=None, op0=MULT)

        def widen_a(c, t, engine):
            w = width_a[c]
            planes = get(("pa", c), [P, T, w], "a_planes%d" % w, 4)
            times_column(engine, planes[:, t, :], a_by[:, t, c : c + w].bitcast(E4M3), a_sc[:, t : t + 1])

        def widen_b(c, g, t, engine):
            w = width_b[c]
            planes = get(("pb", c), [P, T, G * w], "b_planes%d" % w, 3)
            times_column(
                engine, planes[:, t, g * w : (g + 1) * w], b_by[:, g, t, c : c + w].bitcast(E4M3), b_sc[:, g, t : t + 1]
            )

        def interleave(planes, w, key, name, engine="V"):
            mixed = get_mixed(key, T * w)
            copy = nc.scalar.copy if engine == "S" else nc.vector.tensor_copy
            copy(
                out=mixed[:].rearrange("p (c i t) -> p c t i", i=4, t=T),
                in_=planes[:].rearrange("p t (c i) -> p c t i", i=4),
            )

        def quantize(operand, mixed):
            codes, scales = operand
            nc.vector.quantize_mx(out=codes[:].bitcast(FP8X4), scales=scales[:], in_=mixed[:])

        def inter_a(c, engine):
            interleave(tiles["pa", c], width_a[c], ("xa", c), "a_mixed", engine)

        def quant_a(c):
            quantize(a_q[c], tiles["xa", c])

        def inter_b(c):
            interleave(tiles["pb", c], G * width_b[c], ("xb", c), "b_mixed")

        def quant_b(c):
            quantize(b_q[c], tiles["xb", c])

        def inter_f(g, engine):
            mixed = get_mixed(("xf", g), T * BANK)
            copy = nc.scalar.copy if engine == "S" else nc.vector.tensor_copy
            copy(
                out=mixed[:].rearrange("p (t m j) -> p t m j", t=T, j=T),
                in_=f_raw[:, :, g * BANK : (g + 1) * BANK].rearrange("p j (m t) -> p t m j", t=T),
            )

        def quant_f(g):
            quantize(f_q[g], tiles["xf", g])

        def multiply(bank, left, l0, right, r0, w, first=True, last=True):
            nc.tensor.matmul_mx(
                out=bank,
                lhsT=left[0][:, l0 : l0 + P].bitcast(FP8X4),
                lhsT_scale=left[1][:, l0 : l0 + P],
                rhs=right[0][:, r0 : r0 + w].bitcast(FP8X4),
                rhs_scale=right[1][:, r0 : r0 + w],
                start=first,
                stop=last,
            )

        def g_product(c, g, b):
            w = width_a[c]
            if c in TWO_INPUT:
                bank = psum.tile([P, T, P], F32, name="g_bank")
                for t in range(T):
                    multiply(bank[:, t, :], f_q[g], t * P, a_q[c], b * P, P)
            else:
                bank = psum.tile([P, BANK // w, w], F32, name="g_bank")
                for q in range(BANK // w):
                    multiply(bank[:, q, :], f_q[g], (b * (BANK // w) + q) * P, a_q[c], 0, w)
            tiles["gb", c, g, b] = bank

        def g_planes(c, g, b, engine):
            w = width_a[c]
            planes = get(("pg", c), [P, T, G * w], "g_planes%d" % w, 2)
            bank = tiles["gb", c, g, b]
            for q in range(BANK // w):
                t = b * (BANK // w) + q
                times_column(engine, planes[:, t, g * w : (g + 1) * w], bank[:, q, :], v_col[:, g, t : t + 1])

        def g_direct(c, g, b):
            w = width_a[c]
            mixed = get_mixed(("xg", c), T * G * w)
            x0 = T * (g * w + b * P)
            nc.vector.tensor_tensor(
                out=mixed[:, x0 : x0 + T * P].rearrange("p (c i t) -> p c t i", i=4, t=T),
                in0=tiles["gb", c, g, b][:].rearrange("p t (c i) -> p c t i", i=4),
                in1=v_row[:, g : g + 1, :].unsqueeze(3).to_broadcast([P, P // 4, T, 4]),
                op=MULT,
            )

        def inter_g(c):
            w = width_a[c]
            mixed = get_mixed(("xg", c), T * G * w)
            planes = tiles["pg", c]
            nc.vector.tensor_copy(
                out=mixed[:].rearrange("p (c i t) -> p c t i", i=4, t=T),
                in_=planes[:].rearrange("p t (c i) -> p c t i", i=4),
            )

        def quant_g(c):
            quantize(g_q[c], tiles["xg", c])

        def out_product(m, c):
            ca = max(a for a in width_a if a <= m * P)
            w = width_b[c]
            bank = psum.tile([P, BANK], F32, name="out_bank")
            for g in range(G):
                multiply(bank[:, 0:w], g_q[ca], g * width_a[ca] + m * P - ca, b_q[c], g * w, w, g == 0, g == G - 1)
            tiles["ob", m, c] = bank

        def out_block(m, c):
            w = width_b[c]
            if m < WHOLE_ROWS_FROM:
                if ("o", m, c) not in tiles:
                    block = outs.tile([P, w], F32, name="o%d" % w)
                    tiles["o", m, c] = block
                return tiles["o", m, c][:]
            if ("o", m) not in tiles:
                rows = outs.tile([P, N], F32, name="o_rows", bufs=6)
                tiles["o", m] = rows
            return tiles["o", m][:, c : c + w]

        def out_copy(m, c, engine):
            copy = nc.scalar.copy if engine == "S" else nc.vector.tensor_copy
            copy(out=out_block(m, c), in_=tiles["ob", m, c][:, 0 : width_b[c]])

        def add_d(m, c):
            block = out_block(m, c)[:, m * P - c : (m + 1) * P - c]
            nc.vector.scalar_tensor_tensor(
                out=block, in0=ident[:], scalar=d_col[:, m : m + 1], in1=block, op0=MULT, op1=ADD
            )

        def store(m, c):
            nc.sync.dma_start(out=out[m * P : (m + 1) * P, c : c + width_b[c]], in_=out_block(m, c))

        def store_rows(m):
            nc.sync.dma_start(out=out[m * P : (m + 1) * P, :], in_=tiles["o", m][:])

        def v_column():
            nc.vector.tensor_copy(out=v_col[:], in_=v_row[:])

        def d_columns():
            turned = psum.tile([P, P], BF16, name="out_bank")
            nc.tensor.transpose(turned[:], d_row[:], ident[:])
            nc.vector.tensor_copy(out=d_col[:], in_=turned[:, 0:MT])

        actions = {
            "widen_a": widen_a, "widen_b": widen_b, "inter_a": inter_a, "quant_a": quant_a, "inter_b": inter_b,
            "quant_b": quant_b, "inter_f": inter_f, "quant_f": quant_f, "g_product": g_product, "g_planes": g_planes,
            "g_direct": g_direct, "inter_g": inter_g, "quant_g": quant_g, "out_product": out_product,
            "out_copy": out_copy, "add_d": add_d, "store": store, "store_rows": store_rows, "v_column": v_column, "d_columns": d_columns,
        }
        if MANUAL:
            with tc.manual_schedule():
                for step in SEQ:
                    actions[step[0]](*step[1:])
        else:
            for step in SEQ:
                actions[step[0]](*step[1:])
